import numpy as np
import ml_dtypes


def mxq(x, axis, fmt="e4m3"):
    dtype, down = {"e4m3": (ml_dtypes.float8_e4m3fn, 7), "e5m2": (ml_dtypes.float8_e5m2, 14)}[fmt]
    v = np.moveaxis(np.asarray(x, np.float32).astype(ml_dtypes.bfloat16).astype(np.float64), axis, -1)
    blocks = v.reshape(v.shape[:-1] + (-1, 32))
    amax = np.abs(blocks).max(-1, keepdims=True)
    byte = np.maximum(np.where(amax > 0, np.frexp(amax)[1] - 1 + 127, 0) - down, 1)
    scale = np.exp2(byte - 127.0)
    codes = (blocks / scale).astype(np.float32).astype(dtype).astype(np.float64)
    return np.moveaxis((codes * scale).reshape(v.shape), -1, axis)


WIDE = False


def mx_kscale(k, group=512):
    if not WIDE:
        return np.ones(k)
    levels = np.array([10, -10, 5, -5, 0])
    if group != 512:
        return np.exp2(np.random.permutation(np.resize(levels, k // group))).repeat(group)
    if k % 512:
        return np.exp2(np.random.permutation(np.resize(levels, k // 32))).repeat(32)
    a = np.empty((k // 512, 16))
    for p in range(k // 512):
        a[p, :8] = np.random.permutation(np.resize(levels, 8))
        for g in range(8):
            far = levels[np.abs(levels - a[p, g]) >= 10]
            a[p, g + 8] = far[np.random.randint(len(far))]
    return np.exp2(a.ravel()).repeat(32)


def f64(x):
    return np.asarray(x).astype(np.float64)


def striped(idx):
    return np.tile(np.asarray(idx).reshape(-1, 16).T, (8, 1)).astype(np.uint16)


def unstriped(offs):
    return offs[:16].T.reshape(-1).astype(np.int64)


H, KV, D, NQ, N = 4, 2, 256, 512, 512


def setup_inputs():
    n = np.random.standard_normal
    s = mx_kscale(D, 0)[:, None]
    u = mx_kscale(N)
    t = np.random.uniform(0.5, 2.0, N) * u
    v = n((KV, N, 128))
    v[:, :, 127] = 1.0
    return {
        "qT": (n((H, D, NQ)) * s * (0.70 / np.sqrt(D))).astype(np.float32),
        "kT": (n((KV, D, N)) / s).astype(np.float32),
        "t": t.reshape(N, 1).astype(np.float32),
        "v": (v / t[:, None]).astype(np.float32),
        "mask": (np.arange(N)[:, None] <= np.sort(np.random.randint(N // 4, N, NQ))[None, :]).astype(np.float32),
    }


def reference(qT, kT, t, v, mask):
    a = np.repeat(mxq(f64(kT), 1, "e4m3"), H // KV, 0).transpose(0, 2, 1) @ mxq(f64(qT), 1, "e4m3")
    p = np.exp(a)
    p = p * f64(mask)
    w = p * f64(t)
    y = mxq(w, 1, "e4m3").transpose(0, 2, 1) @ np.repeat(mxq(f64(v), 1, "e4m3"), H // KV, 0)
    y = y / (y[:, :, 127:128])
    return y

@@ -1,0 +1,222 @@
+from contextlib import ExitStack
+
+import concourse.mybir as mybir
+
+H, KV, D, NQ, N, E = 4, 2, 256, 512, 512, 128
+FLOPS = 2 * H * N * NQ * D + 2 * H * NQ * N * E
+
+F32 = mybir.dt.float32
+BF16 = mybir.dt.bfloat16
+U32 = mybir.dt.uint32
+U8 = mybir.dt.uint8
+FP8X4 = mybir.dt.float8_e4m3fn_x4
+ACT = mybir.ActivationFunctionType
+ALU = mybir.AluOpType
+
+P = 128
+ROWS = 64
+QB = 128
+PAIRS = ((1, 2), (0, 3))
+K_CHUNKS = ((0, 256), (256, 384), (384, 512))
+M_CHUNKS = ((0, 128), (128, 256), (256, 512))
+
+Q_CHUNKS = ((0, 1), (1, 2), (2, 4), (4, 6), (6, 8))
+
+ORDER = ["lt", "warm", "lq.0", "lk.0", "lk.1", "lk.2", "lq.1", "lm.1", "lq.2", "lm.0", "lm.2", "lq.3", "lv", "lq.4", "iq.0.V", "ik.0.V", "ik.1.V", "Qq.0", "Qk.0.0", "Qk.0.3", "ik.2.2.S", "ik.2.1.V", "Qk.1.1", "Qk.1.0", "iq.1.S", "Qk.0.1", "Qk.1.3", "Qk.1.2", "sc.0.1", "mt.1.S", "sc.0.3", "Qq.1", "sc.0.0", "Qk.0.2", "sc.1.2", "sc.0.2", "sc.1.0", "iq.2.V", "e.0.0", "sc.1.1", "sc.1.3", "mt.0.V", "e.0.1", "Qq.2", "e.1.1", "w.0.0", "sc.2.3", "e.1.0", "w.0.1", "mt.2.S", "sc.3.0", "Qw.0.0", "w.1.2", "sc.2.2", "sc.2.0", "sc.2.1", "sc.3.2", "e.2.0", "Qw.0.1", "sc.3.3", "iq.3.V", "sc.3.1", "e.2.1", "Qw.1.2", "e.3.1", "Qq.3", "iv.1.V", "sc.4.2", "iv.0.S", "w.2.2", "sc.4.1", "sc.4.0", "e.3.0", "sc.4.3", "e.4.0", "Qv", "sc.5.2", "w.3.2", "sc.5.0", "iq.4.S", "pv.1.0", "pv.0.0", "sc.5.1", "sc.5.3", "Qw.2.2", "pv.0.1", "e.4.1", "Qw.3.2", "pv.1.1", "Qq.4", "pv.2.0", "e.5.0", "r.0", "r.1", "sc.6.2", "w.4.2", "e.5.1", "sc.6.0", "sc.6.1", "sc.6.3", "pv.3.1", "w.5.2", "e.6.1", "sc.7.0", "sc.7.3", "e.6.0", "sc.7.2", "pv.2.1", "Qw.4.2", "sc.7.1", "r.2", "w.6.2", "pv.4.1", "e.7.1", "pv.4.0", "pv.3.0", "e.7.0", "Qw.5.2", "f.1.S", "st.1", "r.4", "Qw.6.2", "pv.5.1", "f.0.S", "st.0", "pv.5.0", "r.3", "w.7.1", "pv.6.0", "f.3.S", "st.3", "pv.6.1", "w.7.0", "f.2.S", "st.2", "f.4.S", "st.4", "Qw.7.1", "r.5", "Qw.7.0", "pv.7.1", "f.5.S", "st.5", "r.6", "pv.7.0", "f.6.S", "st.6", "r.7", "f.7.V", "st.7"]
+
+
+def tile_rows_mask_gqa_kernel(tc, qT, kT, t, v, mask, out):
+    nc = tc.nc
+    q_rows = qT.flatten_outer_dims()
+    k_view = kT.flatten_outer_dims().rearrange("(p j) n -> p j n", j=4)
+    v_view = v.rearrange("g (s r) e -> s g r e", r=4)
+    m_view = mask.rearrange("(s r) q -> s r q", r=4)
+    t_view = t.rearrange("(s r) o -> s (r o)", r=4)
+
+    with ExitStack() as ctx:
+        sb = ctx.enter_context(tc.tile_pool(name="sb", bufs=1))
+        ps = ctx.enter_context(tc.psum_pool(name="ps", bufs=1))
+
+        def tile(name, shape, dtype):
+            return sb.tile(shape, dtype, name=name, align_bytes=64)
+
+        warm = tile("warm", [P, 8], F32)
+        warm_out = tile("warm_out", [P, 8], F32)
+        t_sb = tile("t_sb", [P, 4], F32)
+        k_raw = [tile("k_raw%d" % c, [P, 4, b - a], F32) for c, (a, b) in enumerate(K_CHUNKS)]
+        k_bf = tile("k_bf", [P, 4, P, 4], BF16)
+        k_codes = tile("k_codes", [P, 4, P], U32)
+        k_scales = tile("k_scales", [P, 4, P], U8)
+        v_raw = tile("v_raw", [P, KV, 4, E], F32)
+        v_bf = tile("v_bf", [P, KV, E, 4], BF16)
+        v_codes = tile("v_codes", [P, KV * E], U32)
+        v_scales = tile("v_scales", [P, KV * E], U8)
+        m_raw = [tile("m_raw%d" % c, [P, 4, b - a], F32) for c, (a, b) in enumerate(M_CHUNKS)]
+        mt = [tile("mt%d" % c, [P, (b - a) // 4, 4, 4], F32) for c, (a, b) in enumerate(M_CHUNKS)]
+        q_raw = [tile("q_raw%d" % c, [P, 4, (b - a) * QB], F32) for c, (a, b) in enumerate(Q_CHUNKS)]
+        q_bf = [tile("q_bf%d" % c, [P, (b - a) * QB, 4], BF16) for c, (a, b) in enumerate(Q_CHUNKS)]
+        q_codes = [tile("q_codes%d" % c, [P, (b - a) * QB], U32) for c, (a, b) in enumerate(Q_CHUNKS)]
+        q_scales = [tile("q_scales%d" % c, [P, (b - a) * QB], U8) for c, (a, b) in enumerate(Q_CHUNKS)]
+        p_sb = [tile("p%d" % u, [P, 2, QB // 4, 4, 4], F32) for u in range(8)]
+        w_bf = [tile("w_bf%d" % u, [P, 2, QB, 4], BF16) for u in range(8)]
+        w_codes = [tile("w_codes%d" % u, [P, 2, QB], U32) for u in range(8)]
+        w_scales = [tile("w_scales%d" % u, [P, 2, QB], U8) for u in range(8)]
+        rec = [tile("rec%d" % u, [P, 2], F32) for u in range(8)]
+        res = [tile("res%d" % u, [P, 2, E], F32) for u in range(8)]
+        score_banks = [[ps.tile([P, 4, QB], F32, name="score%d_%d" % (g, b)) for b in range(2)] for g in range(2)]
+        y_banks = [ps.tile([P, 4, E], F32, name="y%d" % b) for b in range(4)]
+
+        def copy_on(eng, dst, src):
+            if eng == "V":
+                nc.vector.tensor_copy(out=dst, in_=src)
+            else:
+                nc.scalar.copy(out=dst, in_=src)
+
+        def step(name):
+            word = name.split(".")
+            op = word[0]
+            eng = word[-1]
+            a = int(word[1]) if len(word) > 1 and word[1] not in ("V", "S") else 0
+            b = int(word[2]) if len(word) > 2 and word[2] not in ("V", "S") else 0
+            if op == "warm":
+                nc.vector.memset(warm[:], 0.0)
+                nc.scalar.activation(out=warm_out[:], in_=warm[:], func=ACT.Exp)
+            elif op == "lt":
+                nc.scalar.dma_start(out=t_sb[:], in_=t_view)
+            elif op == "lk":
+                c0, c1 = K_CHUNKS[a]
+                nc.sync.dma_start(out=k_raw[a][:], in_=k_view[:, :, c0:c1])
+            elif op == "lm":
+                c0, c1 = M_CHUNKS[a]
+                nc.sync.dma_start(out=m_raw[a][:], in_=m_view[:, :, c0:c1])
+            elif op == "lv":
+                nc.sync.dma_start(out=v_raw[:], in_=v_view)
+            elif op == "lq":
+                u0, u1 = Q_CHUNKS[a]
+                cols = slice((u0 % 4) * QB, ((u1 - 1) % 4 + 1) * QB)
+                if u0 < 4:
+                    src = q_rows[D : 3 * D, :].rearrange("(p j) n -> p j n", j=4)
+                    nc.sync.dma_start(out=q_raw[a][:], in_=src[:, :, cols])
+                else:
+                    for g in range(2):
+                        h = PAIRS[1][g]
+                        src = q_rows[h * D : (h + 1) * D, :].rearrange("(p j) n -> p j n", j=4)
+                        queue = nc.scalar if (g == 1 and eng == "S") else nc.sync
+                        queue.dma_start(out=q_raw[a][g * ROWS : (g + 1) * ROWS, :, :], in_=src[:, :, cols])
+            elif op == "ik":
+                c0, c1 = K_CHUNKS[a]
+                dst = k_bf[:, :, c0 // 4 : c1 // 4, :].rearrange("p r s j -> p s j r")
+                src = k_raw[a][:].rearrange("p j (s r) -> p s j r", r=4)
+                if b == 0:
+                    copy_on(eng, dst, src)
+                else:
+                    r0 = 2 * (b - 1)
+                    copy_on(eng, dst[:, :, :, r0 : r0 + 2], src[:, :, :, r0 : r0 + 2])
+            elif op == "Qk":
+                s = slice(a * 64, (a + 1) * 64)
+                nc.vector.quantize_mx(
+                    out=k_codes[:, b, s].bitcast(FP8X4),
+                    scales=k_scales[:, b, s],
+                    in_=k_bf[:, b, s, :].rearrange("p s j -> p (s j)"),
+                )
+            elif op == "iv":
+                copy_on(
+                    eng,
+                    v_bf[:, a, :, :].rearrange("p (c i) r -> p c r i", i=4),
+                    v_raw[:, a, :, :].rearrange("p r (c i) -> p c r i", i=4),
+                )
+            elif op == "Qv":
+                nc.vector.quantize_mx(
+                    out=v_codes[:].bitcast(FP8X4), scales=v_scales[:], in_=v_bf[:].rearrange("p g e r -> p (g e r)")
+                )
+            elif op == "mt":
+                for r in range(4):
+                    if eng == "V":
+                        nc.vector.tensor_scalar(
+                            out=mt[a][:, :, r, :], in0=m_raw[a][:, r, :].rearrange("p (c i) -> p c i", i=4), scalar1=t_sb[:, r : r + 1], scalar2=None, op0=ALU.mult
+                        )
+                    else:
+                        nc.scalar.activation(out=mt[a][:, :, r, :], in_=m_raw[a][:, r, :].rearrange("p (c i) -> p c i", i=4), func=ACT.Copy, scale=t_sb[:, r : r + 1])
+            elif op == "iq":
+                copy_on(
+                    eng,
+                    q_bf[a][:].rearrange("p (c i) j -> p c j i", i=4),
+                    q_raw[a][:].rearrange("p j (c i) -> p c j i", i=4),
+                )
+            elif op == "Qq":
+                nc.vector.quantize_mx(
+                    out=q_codes[a][:].bitcast(FP8X4), scales=q_scales[a][:], in_=q_bf[a][:].rearrange("p n j -> p (n j)")
+                )
+            elif op == "sc":
+                c = [i for i, (u0, u1) in enumerate(Q_CHUNKS) if u0 <= a < u1][0]
+                cols = slice((a - Q_CHUNKS[c][0]) * QB, (a - Q_CHUNKS[c][0] + 1) * QB)
+                for g in range(2):
+                    rows = slice(g * ROWS, (g + 1) * ROWS)
+                    nc.tensor.matmul_mx(
+                        out=score_banks[g][a % 2][:, b, :],
+                        lhsT=k_codes[rows, b, :].bitcast(FP8X4),
+                        lhsT_scale=k_scales[rows, b, :],
+                        rhs=q_codes[c][rows, cols].bitcast(FP8X4),
+                        rhs_scale=q_scales[c][rows, cols],
+                        start=True,
+                        stop=True,
+                    )
+            elif op == "e":
+                nc.scalar.activation(
+                    out=p_sb[a][:, b],
+                    in_=score_banks[b][a % 2][:].rearrange("p r (c i) -> p c r i", i=4),
+                    func=ACT.Exp,
+                )
+            elif op == "w":
+                q0 = (a % 4) * QB
+                c = [i for i, (c0, c1) in enumerate(M_CHUNKS) if c0 <= q0 < c1][0]
+                c0 = (q0 - M_CHUNKS[c][0]) // 4
+                heads = slice(0, 2) if b == 2 else slice(b, b + 1)
+                count = 2 if b == 2 else 1
+                nc.vector.tensor_tensor(
+                    out=w_bf[a][:, heads].rearrange("p g (c i) r -> p g c r i", i=4),
+                    in0=p_sb[a][:, heads],
+                    in1=mt[c][:, c0 : c0 + QB // 4].unsqueeze(1).to_broadcast([P, count, QB // 4, 4, 4]),
+                    op=ALU.mult,
+                )
+            elif op == "Qw":
+                heads = slice(0, 2) if b == 2 else slice(b, b + 1)
+                nc.vector.quantize_mx(
+                    out=w_codes[a][:, heads].rearrange("p g n -> p (g n)").bitcast(FP8X4),
+                    scales=w_scales[a][:, heads].rearrange("p g n -> p (g n)"),
+                    in_=w_bf[a][:, heads].rearrange("p g n r -> p (g n r)"),
+                )
+            elif op == "pv":
+                cols = slice(b * E, (b + 1) * E)
+                nc.tensor.matmul_mx(
+                    out=y_banks[a % 4][:, 2 * (a // 4) + b, :],
+                    lhsT=w_codes[a][:, b, :].bitcast(FP8X4),
+                    lhsT_scale=w_scales[a][:, b, :],
+                    rhs=v_codes[:, cols].bitcast(FP8X4),
+                    rhs_scale=v_scales[:, cols],
+                    start=True,
+                    stop=True,
+                )
+            elif op == "r":
+                nc.vector.reciprocal(out=rec[a][:], in_=y_banks[a % 4][:, 2 * (a // 4) : 2 * (a // 4) + 2, E - 1])
+            elif op == "f":
+                if eng == "V":
+                    nc.vector.tensor_tensor(
+                        out=res[a][:],
+                        in0=y_banks[a % 4][:, 2 * (a // 4) : 2 * (a // 4) + 2, :],
+                        in1=rec[a][:].unsqueeze(2).to_broadcast([P, 2, E]),
+                        op=ALU.mult,
+                    )
+                else:
+                    for g in range(2):
+                        nc.scalar.activation(
+                            out=res[a][:, g, :], in_=y_banks[a % 4][:, 2 * (a // 4) + g, :], func=ACT.Copy, scale=rec[a][:, g : g + 1]
+                        )
+            else:
+                h0, h1 = PAIRS[a // 4]
+                dst = out[h0 : h1 + 1 : h1 - h0, (a % 4) * QB : (a % 4 + 1) * QB, :].rearrange("h q e -> q h e")
+                nc.sync.dma_start(out=dst, in_=res[a][:])
+
+        with tc.manual_schedule():
+            for name in ORDER:
+                step(name)

@@ -15,23 +15,28 @@ ALU = mybir.AluOpType
 
 P = 128
 ROWS = 64
+PACK = 4
 QB = 128
+RUN = 4
+BLOCKS = NQ // QB
+UNITS = 2 * BLOCKS
+JOBS = 2 * UNITS
+LAST = UNITS - 1
+
 PAIRS = ((1, 2), (0, 3))
-K_CHUNKS = ((0, 256), (256, 384), (384, 512))
-M_CHUNKS = ((0, 128), (128, 256), (256, 512))
-
-Q_CHUNKS = ((0, 1), (1, 2), (2, 4), (4, 6), (6, 8))
-
-ORDER = ["lt", "warm", "lq.0", "lk.0", "lk.1", "lk.2", "lq.1", "lm.1", "lq.2", "lm.0", "lm.2", "lq.3", "lv", "lq.4", "iq.0.V", "ik.0.V", "ik.1.V", "Qq.0", "Qk.0.0", "Qk.0.3", "ik.2.2.S", "ik.2.1.V", "Qk.1.1", "Qk.1.0", "iq.1.S", "Qk.0.1", "Qk.1.3", "Qk.1.2", "sc.0.1", "mt.1.S", "sc.0.3", "Qq.1", "sc.0.0", "Qk.0.2", "sc.1.2", "sc.0.2", "sc.1.0", "iq.2.V", "e.0.0", "sc.1.1", "sc.1.3", "mt.0.V", "e.0.1", "Qq.2", "e.1.1", "w.0.0", "sc.2.3", "e.1.0", "w.0.1", "mt.2.S", "sc.3.0", "Qw.0.0", "w.1.2", "sc.2.2", "sc.2.0", "sc.2.1", "sc.3.2", "e.2.0", "Qw.0.1", "sc.3.3", "iq.3.V", "sc.3.1", "e.2.1", "Qw.1.2", "e.3.1", "Qq.3", "iv.1.V", "sc.4.2", "iv.0.S", "w.2.2", "sc.4.1", "sc.4.0", "e.3.0", "sc.4.3", "e.4.0", "Qv", "sc.5.2", "w.3.2", "sc.5.0", "iq.4.S", "pv.1.0", "pv.0.0", "sc.5.1", "sc.5.3", "Qw.2.2", "pv.0.1", "e.4.1", "Qw.3.2", "pv.1.1", "Qq.4", "pv.2.0", "e.5.0", "r.0", "r.1", "sc.6.2", "w.4.2", "e.5.1", "sc.6.0", "sc.6.1", "sc.6.3", "pv.3.1", "w.5.2", "e.6.1", "sc.7.0", "sc.7.3", "e.6.0", "sc.7.2", "pv.2.1", "Qw.4.2", "sc.7.1", "r.2", "w.6.2", "pv.4.1", "e.7.1", "pv.4.0", "pv.3.0", "e.7.0", "Qw.5.2", "f.1.S", "st.1", "r.4", "Qw.6.2", "pv.5.1", "f.0.S", "st.0", "pv.5.0", "r.3", "w.7.1", "pv.6.0", "f.3.S", "st.3", "pv.6.1", "w.7.0", "f.2.S", "st.2", "f.4.S", "st.4", "Qw.7.1", "r.5", "Qw.7.0", "pv.7.1", "f.5.S", "st.5", "r.6", "pv.7.0", "f.6.S", "st.6", "r.7", "f.7.V", "st.7"]
+Q_GROUPS = ((0, 1), (1, 2), (2, 4), (4, 6), (6, 8))
+M_GROUPS = ((0, 128), (128, 256), (256, 512))
+HALF = P // 2
+K_SHARE = 44
 
 
 def tile_rows_mask_gqa_kernel(tc, qT, kT, t, v, mask, out):
     nc = tc.nc
     q_rows = qT.flatten_outer_dims()
-    k_view = kT.flatten_outer_dims().rearrange("(p j) n -> p j n", j=4)
-    v_view = v.rearrange("g (s r) e -> s g r e", r=4)
-    m_view = mask.rearrange("(s r) q -> s r q", r=4)
-    t_view = t.rearrange("(s r) o -> s (r o)", r=4)
+    k_view = kT.flatten_outer_dims().rearrange("(p j) n -> p j n", j=PACK)
+    v_view = v.rearrange("g (s r) e -> s g r e", r=PACK)
+    m_view = mask.rearrange("(s r) q -> s r q", r=PACK)
+    t_view = t.rearrange("(s r) o -> s (r o)", r=PACK)
 
     with ExitStack() as ctx:
         sb = ctx.enter_context(tc.tile_pool(name="sb", bufs=1))
@@ -40,183 +45,244 @@ def tile_rows_mask_gqa_kernel(tc, qT, kT, t, v, mask, out):
         def tile(name, shape, dtype):
             return sb.tile(shape, dtype, name=name, align_bytes=64)
 
-        warm = tile("warm", [P, 8], F32)
-        warm_out = tile("warm_out", [P, 8], F32)
-        t_sb = tile("t_sb", [P, 4], F32)
-        k_raw = [tile("k_raw%d" % c, [P, 4, b - a], F32) for c, (a, b) in enumerate(K_CHUNKS)]
-        k_bf = tile("k_bf", [P, 4, P, 4], BF16)
-        k_codes = tile("k_codes", [P, 4, P], U32)
-        k_scales = tile("k_scales", [P, 4, P], U8)
-        v_raw = tile("v_raw", [P, KV, 4, E], F32)
-        v_bf = tile("v_bf", [P, KV, E, 4], BF16)
+        t_sb = tile("t_sb", [P, PACK], F32)
+        k_raw = [tile("k_raw%d" % half, [P, PACK, N // 2], F32) for half in range(2)]
+        k_bf = tile("k_bf", [P, PACK, P, PACK], BF16)
+        k_codes = tile("k_codes", [P, PACK, P], U32)
+        k_scales = tile("k_scales", [P, PACK, P], U8)
+        v_raw = tile("v_raw", [P, KV, PACK, E], F32)
+        v_bf = tile("v_bf", [P, KV, E, PACK], BF16)
         v_codes = tile("v_codes", [P, KV * E], U32)
         v_scales = tile("v_scales", [P, KV * E], U8)
-        m_raw = [tile("m_raw%d" % c, [P, 4, b - a], F32) for c, (a, b) in enumerate(M_CHUNKS)]
-        mt = [tile("mt%d" % c, [P, (b - a) // 4, 4, 4], F32) for c, (a, b) in enumerate(M_CHUNKS)]
-        q_raw = [tile("q_raw%d" % c, [P, 4, (b - a) * QB], F32) for c, (a, b) in enumerate(Q_CHUNKS)]
-        q_bf = [tile("q_bf%d" % c, [P, (b - a) * QB, 4], BF16) for c, (a, b) in enumerate(Q_CHUNKS)]
-        q_codes = [tile("q_codes%d" % c, [P, (b - a) * QB], U32) for c, (a, b) in enumerate(Q_CHUNKS)]
-        q_scales = [tile("q_scales%d" % c, [P, (b - a) * QB], U8) for c, (a, b) in enumerate(Q_CHUNKS)]
-        p_sb = [tile("p%d" % u, [P, 2, QB // 4, 4, 4], F32) for u in range(8)]
-        w_bf = [tile("w_bf%d" % u, [P, 2, QB, 4], BF16) for u in range(8)]
-        w_codes = [tile("w_codes%d" % u, [P, 2, QB], U32) for u in range(8)]
-        w_scales = [tile("w_scales%d" % u, [P, 2, QB], U8) for u in range(8)]
-        rec = [tile("rec%d" % u, [P, 2], F32) for u in range(8)]
-        res = [tile("res%d" % u, [P, 2, E], F32) for u in range(8)]
-        score_banks = [[ps.tile([P, 4, QB], F32, name="score%d_%d" % (g, b)) for b in range(2)] for g in range(2)]
+        m_raw = [tile("m_raw%d" % c, [P, PACK, b - a], F32) for c, (a, b) in enumerate(M_GROUPS)]
+        mask_t = tile("mask_t", [P, PACK, NQ], F32)
+        q_raw = [tile("q_raw%d" % c, [P, PACK, (b - a) * QB], F32) for c, (a, b) in enumerate(Q_GROUPS)]
+        q_bf = [tile("q_bf%d" % c, [P, (b - a) * QB, PACK], BF16) for c, (a, b) in enumerate(Q_GROUPS)]
+        q_codes = [tile("q_codes%d" % c, [P, (b - a) * QB], U32) for c, (a, b) in enumerate(Q_GROUPS)]
+        q_scales = [tile("q_scales%d" % c, [P, (b - a) * QB], U8) for c, (a, b) in enumerate(Q_GROUPS)]
+        probs = [tile("probs%d" % n, [P, QB // RUN, PACK, RUN], F32) for n in range(JOBS)]
+        w_bf = [tile("w_bf%d" % u, [P, 2, QB, PACK], BF16) for u in range(UNITS)]
+        w_codes = [tile("w_codes%d" % u, [P, 2 * QB], U32) for u in range(UNITS)]
+        w_scales = [tile("w_scales%d" % u, [P, 2 * QB], U8) for u in range(UNITS)]
+        recips = tile("recips", [P, JOBS], F32)
+        result = tile("result", [P, JOBS, E], F32)
+        score_banks = [[ps.tile([P, PACK, QB], F32, name="score%d_%d" % (g, b)) for b in range(2)] for g in range(2)]
         y_banks = [ps.tile([P, 4, E], F32, name="y%d" % b) for b in range(4)]
 
-        def copy_on(eng, dst, src):
-            if eng == "V":
+        def y_of(first, count):
+            if first >= 2 * LAST:
+                return y_banks[first - 2 * LAST][:, 0:count, :]
+            return y_banks[first // 4][:, first % 4 : first % 4 + count, :]
+
+        def copy(engine, dst, src):
+            if engine == "vector":
                 nc.vector.tensor_copy(out=dst, in_=src)
             else:
                 nc.scalar.copy(out=dst, in_=src)
 
-        def step(name):
-            word = name.split(".")
-            op = word[0]
-            eng = word[-1]
-            a = int(word[1]) if len(word) > 1 and word[1] not in ("V", "S") else 0
-            b = int(word[2]) if len(word) > 2 and word[2] not in ("V", "S") else 0
-            if op == "warm":
-                nc.vector.memset(warm[:], 0.0)
-                nc.scalar.activation(out=warm_out[:], in_=warm[:], func=ACT.Exp)
-            elif op == "lt":
-                nc.scalar.dma_start(out=t_sb[:], in_=t_view)
-            elif op == "lk":
-                c0, c1 = K_CHUNKS[a]
-                nc.sync.dma_start(out=k_raw[a][:], in_=k_view[:, :, c0:c1])
-            elif op == "lm":
-                c0, c1 = M_CHUNKS[a]
-                nc.sync.dma_start(out=m_raw[a][:], in_=m_view[:, :, c0:c1])
-            elif op == "lv":
-                nc.sync.dma_start(out=v_raw[:], in_=v_view)
-            elif op == "lq":
-                u0, u1 = Q_CHUNKS[a]
-                cols = slice((u0 % 4) * QB, ((u1 - 1) % 4 + 1) * QB)
-                if u0 < 4:
-                    src = q_rows[D : 3 * D, :].rearrange("(p j) n -> p j n", j=4)
-                    nc.sync.dma_start(out=q_raw[a][:], in_=src[:, :, cols])
+        def quantise(codes, scales, src):
+            nc.vector.quantize_mx(out=codes.bitcast(FP8X4), scales=scales, in_=src)
+
+        def load_k(half):
+            nc.sync.dma_start(out=k_raw[half][:], in_=k_view[:, :, half * N // 2 : (half + 1) * N // 2])
+
+        def load_q(c):
+            u0, u1 = Q_GROUPS[c]
+            cols = slice((u0 % BLOCKS) * QB, ((u1 - 1) % BLOCKS + 1) * QB)
+            heads = PAIRS[u0 // BLOCKS]
+            if heads[1] == heads[0] + 1:
+                src = q_rows[heads[0] * D : (heads[1] + 1) * D, :].rearrange("(p j) n -> p j n", j=PACK)
+                nc.sync.dma_start(out=q_raw[c][:], in_=src[:, :, cols])
+            else:
+                for g, h in enumerate(heads):
+                    src = q_rows[h * D : (h + 1) * D, :].rearrange("(p j) n -> p j n", j=PACK)
+                    nc.sync.dma_start(out=q_raw[c][g * ROWS : (g + 1) * ROWS, :, :], in_=src[:, :, cols])
+
+        def load_mask(c):
+            nc.sync.dma_start(out=m_raw[c][:], in_=m_view[:, :, M_GROUPS[c][0] : M_GROUPS[c][1]])
+
+        def deal_k(engine, half, s0, s1):
+            dst = k_bf[:, :, half * HALF + s0 : half * HALF + s1, :].rearrange("p r s j -> p s j r")
+            src = k_raw[half][:].rearrange("p j (s r) -> p s j r", r=PACK)
+            copy(engine, dst, src[:, s0:s1])
+
+        def quantise_k(half):
+            s = slice(half * HALF, (half + 1) * HALF)
+            for r in range(PACK):
+                quantise(k_codes[:, r, s], k_scales[:, r, s], k_bf[:, r, s, :].rearrange("p s j -> p (s j)"))
+
+        def interleave_q(engine, c):
+            copy(
+                engine,
+                q_bf[c][:].rearrange("p (c i) j -> p c j i", i=RUN),
+                q_raw[c][:].rearrange("p j (c i) -> p c j i", i=RUN),
+            )
+
+        def quantise_q(c):
+            quantise(q_codes[c][:], q_scales[c][:], q_bf[c][:].rearrange("p n j -> p (n j)"))
+
+        def interleave_v(engine):
+            for g in range(KV):
+                copy(
+                    engine,
+                    v_bf[:, g, :, :].rearrange("p (c i) r -> p c r i", i=RUN),
+                    v_raw[:, g, :, :].rearrange("p r (c i) -> p c r i", i=RUN),
+                )
+
+        def quantise_v():
+            quantise(v_codes[:], v_scales[:], v_bf[:].rearrange("p g e r -> p (g e r)"))
+
+        def scale_mask(engine, c):
+            q0, q1 = M_GROUPS[c]
+            for r in range(PACK):
+                dst, src, factor = mask_t[:, r, q0:q1], m_raw[c][:, r, :], t_sb[:, r : r + 1]
+                if engine == "vector":
+                    nc.vector.tensor_scalar(out=dst, in0=src, scalar1=factor, scalar2=None, op0=ALU.mult)
                 else:
-                    for g in range(2):
-                        h = PAIRS[1][g]
-                        src = q_rows[h * D : (h + 1) * D, :].rearrange("(p j) n -> p j n", j=4)
-                        queue = nc.scalar if (g == 1 and eng == "S") else nc.sync
-                        queue.dma_start(out=q_raw[a][g * ROWS : (g + 1) * ROWS, :, :], in_=src[:, :, cols])
-            elif op == "ik":
-                c0, c1 = K_CHUNKS[a]
-                dst = k_bf[:, :, c0 // 4 : c1 // 4, :].rearrange("p r s j -> p s j r")
-                src = k_raw[a][:].rearrange("p j (s r) -> p s j r", r=4)
-                if b == 0:
-                    copy_on(eng, dst, src)
-                else:
-                    r0 = 2 * (b - 1)
-                    copy_on(eng, dst[:, :, :, r0 : r0 + 2], src[:, :, :, r0 : r0 + 2])
-            elif op == "Qk":
-                s = slice(a * 64, (a + 1) * 64)
-                nc.vector.quantize_mx(
-                    out=k_codes[:, b, s].bitcast(FP8X4),
-                    scales=k_scales[:, b, s],
-                    in_=k_bf[:, b, s, :].rearrange("p s j -> p (s j)"),
-                )
-            elif op == "iv":
-                copy_on(
-                    eng,
-                    v_bf[:, a, :, :].rearrange("p (c i) r -> p c r i", i=4),
-                    v_raw[:, a, :, :].rearrange("p r (c i) -> p c r i", i=4),
-                )
-            elif op == "Qv":
-                nc.vector.quantize_mx(
-                    out=v_codes[:].bitcast(FP8X4), scales=v_scales[:], in_=v_bf[:].rearrange("p g e r -> p (g e r)")
-                )
-            elif op == "mt":
-                for r in range(4):
-                    if eng == "V":
-                        nc.vector.tensor_scalar(
-                            out=mt[a][:, :, r, :], in0=m_raw[a][:, r, :].rearrange("p (c i) -> p c i", i=4), scalar1=t_sb[:, r : r + 1], scalar2=None, op0=ALU.mult
-                        )
-                    else:
-                        nc.scalar.activation(out=mt[a][:, :, r, :], in_=m_raw[a][:, r, :].rearrange("p (c i) -> p c i", i=4), func=ACT.Copy, scale=t_sb[:, r : r + 1])
-            elif op == "iq":
-                copy_on(
-                    eng,
-                    q_bf[a][:].rearrange("p (c i) j -> p c j i", i=4),
-                    q_raw[a][:].rearrange("p j (c i) -> p c j i", i=4),
-                )
-            elif op == "Qq":
-                nc.vector.quantize_mx(
-                    out=q_codes[a][:].bitcast(FP8X4), scales=q_scales[a][:], in_=q_bf[a][:].rearrange("p n j -> p (n j)")
-                )
-            elif op == "sc":
-                c = [i for i, (u0, u1) in enumerate(Q_CHUNKS) if u0 <= a < u1][0]
-                cols = slice((a - Q_CHUNKS[c][0]) * QB, (a - Q_CHUNKS[c][0] + 1) * QB)
+                    nc.scalar.activation(out=dst, in_=src, func=ACT.Copy, scale=factor)
+
+        def scores(u):
+            c = [c for c, (u0, u1) in enumerate(Q_GROUPS) if u0 <= u < u1][0]
+            cols = slice((u - Q_GROUPS[c][0]) * QB, (u - Q_GROUPS[c][0] + 1) * QB)
+            for r in range(PACK):
                 for g in range(2):
                     rows = slice(g * ROWS, (g + 1) * ROWS)
                     nc.tensor.matmul_mx(
-                        out=score_banks[g][a % 2][:, b, :],
-                        lhsT=k_codes[rows, b, :].bitcast(FP8X4),
-                        lhsT_scale=k_scales[rows, b, :],
+                        out=score_banks[g][u % 2][:, r, :],
+                        lhsT=k_codes[rows, r, :].bitcast(FP8X4),
+                        lhsT_scale=k_scales[rows, r, :],
                         rhs=q_codes[c][rows, cols].bitcast(FP8X4),
                         rhs_scale=q_scales[c][rows, cols],
                         start=True,
                         stop=True,
                     )
-            elif op == "e":
-                nc.scalar.activation(
-                    out=p_sb[a][:, b],
-                    in_=score_banks[b][a % 2][:].rearrange("p r (c i) -> p c r i", i=4),
-                    func=ACT.Exp,
-                )
-            elif op == "w":
-                q0 = (a % 4) * QB
-                c = [i for i, (c0, c1) in enumerate(M_CHUNKS) if c0 <= q0 < c1][0]
-                c0 = (q0 - M_CHUNKS[c][0]) // 4
-                heads = slice(0, 2) if b == 2 else slice(b, b + 1)
-                count = 2 if b == 2 else 1
-                nc.vector.tensor_tensor(
-                    out=w_bf[a][:, heads].rearrange("p g (c i) r -> p g c r i", i=4),
-                    in0=p_sb[a][:, heads],
-                    in1=mt[c][:, c0 : c0 + QB // 4].unsqueeze(1).to_broadcast([P, count, QB // 4, 4, 4]),
-                    op=ALU.mult,
-                )
-            elif op == "Qw":
-                heads = slice(0, 2) if b == 2 else slice(b, b + 1)
-                nc.vector.quantize_mx(
-                    out=w_codes[a][:, heads].rearrange("p g n -> p (g n)").bitcast(FP8X4),
-                    scales=w_scales[a][:, heads].rearrange("p g n -> p (g n)"),
-                    in_=w_bf[a][:, heads].rearrange("p g n r -> p (g n r)"),
-                )
-            elif op == "pv":
-                cols = slice(b * E, (b + 1) * E)
+
+        def exponentiate(n):
+            bank = score_banks[n % 2][n // 2 % 2]
+            nc.scalar.activation(out=probs[n][:], in_=bank[:].rearrange("p r (c i) -> p c r i", i=RUN), func=ACT.Exp)
+
+        def weigh(n):
+            q0 = (n // 2 % BLOCKS) * QB
+            nc.vector.tensor_tensor(
+                out=w_bf[n // 2][:, n % 2].rearrange("p (c i) r -> p c r i", i=RUN),
+                in0=probs[n][:],
+                in1=mask_t[:, :, q0 : q0 + QB].rearrange("p r (c i) -> p c r i", i=RUN),
+                op=ALU.mult,
+            )
+
+        def quantise_w(first, count):
+            u, g = divmod(first, 2)
+            cols = slice(g * QB, (g + count) * QB)
+            quantise(w_codes[u][:, cols], w_scales[u][:, cols], w_bf[u][:, g : g + count].rearrange("p g n r -> p (g n r)"))
+
+        def mix_values(first, count):
+            for n in range(first, first + count):
+                u, g = divmod(n, 2)
                 nc.tensor.matmul_mx(
-                    out=y_banks[a % 4][:, 2 * (a // 4) + b, :],
-                    lhsT=w_codes[a][:, b, :].bitcast(FP8X4),
-                    lhsT_scale=w_scales[a][:, b, :],
-                    rhs=v_codes[:, cols].bitcast(FP8X4),
-                    rhs_scale=v_scales[:, cols],
+                    out=y_of(n, 1)[:, 0, :],
+                    lhsT=w_codes[u][:, g * QB : (g + 1) * QB].bitcast(FP8X4),
+                    lhsT_scale=w_scales[u][:, g * QB : (g + 1) * QB],
+                    rhs=v_codes[:, g * E : (g + 1) * E].bitcast(FP8X4),
+                    rhs_scale=v_scales[:, g * E : (g + 1) * E],
                     start=True,
                     stop=True,
                 )
-            elif op == "r":
-                nc.vector.reciprocal(out=rec[a][:], in_=y_banks[a % 4][:, 2 * (a // 4) : 2 * (a // 4) + 2, E - 1])
-            elif op == "f":
-                if eng == "V":
-                    nc.vector.tensor_tensor(
-                        out=res[a][:],
-                        in0=y_banks[a % 4][:, 2 * (a // 4) : 2 * (a // 4) + 2, :],
-                        in1=rec[a][:].unsqueeze(2).to_broadcast([P, 2, E]),
-                        op=ALU.mult,
-                    )
-                else:
-                    for g in range(2):
-                        nc.scalar.activation(
-                            out=res[a][:, g, :], in_=y_banks[a % 4][:, 2 * (a // 4) + g, :], func=ACT.Copy, scale=rec[a][:, g : g + 1]
-                        )
+
+        def invert(first, count):
+            nc.vector.reciprocal(out=recips[:, first : first + count], in_=y_of(first, count)[:, :, E - 1])
+
+        def finish(engine, first, count):
+            jobs = slice(first, first + count)
+            if engine == "vector":
+                factor = recips[:, jobs].unsqueeze(2).to_broadcast([P, count, E])
+                nc.vector.tensor_tensor(out=result[:, jobs, :], in0=y_of(first, count), in1=factor, op=ALU.mult)
             else:
-                h0, h1 = PAIRS[a // 4]
-                dst = out[h0 : h1 + 1 : h1 - h0, (a % 4) * QB : (a % 4 + 1) * QB, :].rearrange("h q e -> q h e")
-                nc.sync.dma_start(out=dst, in_=res[a][:])
+                for n in range(first, first + count):
+                    nc.scalar.activation(out=result[:, n, :], in_=y_of(n, 1)[:, 0, :], func=ACT.Copy, scale=recips[:, n : n + 1])
+            u, g = divmod(first, 2)
+            h0, h1 = PAIRS[u // BLOCKS]
+            q0 = (u % BLOCKS) * QB
+            dst = out[h0 : h1 + 1 : h1 - h0, q0 : q0 + QB, :].rearrange("h q e -> q h e")
+            nc.sync.dma_start(out=dst[:, g : g + count, :], in_=result[:, jobs, :])
+
+        before_exp = {
+            2: [(scale_mask, "scalar", 1)],
+            5: [(interleave_q, "scalar", 3)],
+            8: [(interleave_v, "scalar")],
+            9: [(interleave_q, "scalar", 4)],
+            12: [(finish, "scalar", 0, 2)],
+            14: [(finish, "scalar", 2, 2)],
+        }
+        before_weigh = {
+            0: [(interleave_q, "vector", 2), (scale_mask, "vector", 0), (quantise_q, 2)],
+            4: [(quantise_w, 0, 2), (quantise_w, 2, 2), (scale_mask, "vector", 2), (quantise_q, 3)],
+            7: [(quantise_w, 4, 2), (quantise_v,)],
+            9: [(quantise_w, 6, 2), (quantise_q, 4), (invert, 0, 4)],
+            12: [(quantise_w, 8, 2), (quantise_w, 10, 2)],
+            14: [(invert, 4, 4), (quantise_w, 12, 1)],
+            15: [(quantise_w, 13, 1), (invert, 8, 4)],
+        }
+        after_weigh = {
+            0: [(scores, 2)],
+            2: [(scores, 3)],
+            4: [(scores, 4)],
+            6: [(scores, 5)],
+            7: [(mix_values, 0, 6)],
+            9: [(scores, 6)],
+            10: [(scores, 7), (mix_values, 6, 2)],
+            12: [(mix_values, 8, 4)],
+            14: [(mix_values, 12, 1)],
+            15: [(mix_values, 13, 1)],
+        }
+
+        def run(steps):
+            for fn, *args in steps:
+                fn(*args)
 
         with tc.manual_schedule():
-            for name in ORDER:
-                step(name)
+            nc.scalar.dma_start(out=t_sb[:], in_=t_view)
+
+            load_k(0)
+            load_q(0)
+            load_k(1)
+            load_q(1)
+            load_q(2)
+            load_mask(0)
+            load_mask(1)
+            load_q(3)
+            load_mask(2)
+            nc.sync.dma_start(out=v_raw[:], in_=v_view)
+            load_q(4)
+
+            deal_k("vector", 0, 0, HALF)
+            quantise_k(0)
+            interleave_q("scalar", 0)
+            deal_k("vector", 1, 0, K_SHARE)
+            deal_k("scalar", 1, K_SHARE, HALF)
+            quantise_q(0)
+            quantise_k(1)
+            scores(0)
+            interleave_q("scalar", 1)
+            quantise_q(1)
+            scores(1)
+            exponentiate(0)
+
+            for n in range(JOBS):
+                if n + 1 < JOBS:
+                    run(before_exp.get(n + 1, []))
+                    exponentiate(n + 1)
+                run(before_weigh.get(n, []))
+                weigh(n)
+                run(after_weigh.get(n, []))
+
+            for u in range(2, LAST - 1):
+                finish("scalar", 2 * u, 2)
+            quantise_w(JOBS - 2, 1)
+            mix_values(JOBS - 2, 1)
+            invert(JOBS - 4, 2)
+            quantise_w(JOBS - 1, 1)
+            mix_values(JOBS - 1, 1)
+            finish("vector", JOBS - 4, 2)
+            for n in (JOBS - 2, JOBS - 1):
+                invert(n, 1)
+                finish("scalar", n, 1)

from contextlib import ExitStack

import concourse.mybir as mybir

H, KV, D, NQ, N, E = 4, 2, 256, 512, 512, 128
FLOPS = 2 * H * N * NQ * D + 2 * H * NQ * N * E

F32 = mybir.dt.float32
BF16 = mybir.dt.bfloat16
U32 = mybir.dt.uint32
U8 = mybir.dt.uint8
FP8X4 = mybir.dt.float8_e4m3fn_x4
ACT = mybir.ActivationFunctionType
ALU = mybir.AluOpType

P = 128
ROWS = 64
PACK = 4
QB = 128
RUN = 4
BLOCKS = NQ // QB
UNITS = 2 * BLOCKS
JOBS = 2 * UNITS
LAST = UNITS - 1

PAIRS = ((1, 2), (0, 3))
Q_GROUPS = ((0, 1), (1, 2), (2, 4), (4, 6), (6, 8))
M_GROUPS = ((0, 128), (128, 256), (256, 512))
HALF = P // 2
K_SHARE = 44


def tile_rows_mask_gqa_kernel(tc, qT, kT, t, v, mask, out):
    nc = tc.nc
    q_rows = qT.flatten_outer_dims()
    k_view = kT.flatten_outer_dims().rearrange("(p j) n -> p j n", j=PACK)
    v_view = v.rearrange("g (s r) e -> s g r e", r=PACK)
    m_view = mask.rearrange("(s r) q -> s r q", r=PACK)
    t_view = t.rearrange("(s r) o -> s (r o)", r=PACK)

    with ExitStack() as ctx:
        sb = ctx.enter_context(tc.tile_pool(name="sb", bufs=1))
        ps = ctx.enter_context(tc.psum_pool(name="ps", bufs=1))

        def tile(name, shape, dtype):
            return sb.tile(shape, dtype, name=name, align_bytes=64)

        t_sb = tile("t_sb", [P, PACK], F32)
        k_raw = [tile("k_raw%d" % half, [P, PACK, N // 2], F32) for half in range(2)]
        k_bf = tile("k_bf", [P, PACK, P, PACK], BF16)
        k_codes = tile("k_codes", [P, PACK, P], U32)
        k_scales = tile("k_scales", [P, PACK, P], U8)
        v_raw = tile("v_raw", [P, KV, PACK, E], F32)
        v_bf = tile("v_bf", [P, KV, E, PACK], BF16)
        v_codes = tile("v_codes", [P, KV * E], U32)
        v_scales = tile("v_scales", [P, KV * E], U8)
        m_raw = [tile("m_raw%d" % c, [P, PACK, b - a], F32) for c, (a, b) in enumerate(M_GROUPS)]
        mask_t = tile("mask_t", [P, PACK, NQ], F32)
        q_raw = [tile("q_raw%d" % c, [P, PACK, (b - a) * QB], F32) for c, (a, b) in enumerate(Q_GROUPS)]
        q_bf = [tile("q_bf%d" % c, [P, (b - a) * QB, PACK], BF16) for c, (a, b) in enumerate(Q_GROUPS)]
        q_codes = [tile("q_codes%d" % c, [P, (b - a) * QB], U32) for c, (a, b) in enumerate(Q_GROUPS)]
        q_scales = [tile("q_scales%d" % c, [P, (b - a) * QB], U8) for c, (a, b) in enumerate(Q_GROUPS)]
        probs = [tile("probs%d" % n, [P, QB // RUN, PACK, RUN], F32) for n in range(JOBS)]
        w_bf = [tile("w_bf%d" % u, [P, 2, QB, PACK], BF16) for u in range(UNITS)]
        w_codes = [tile("w_codes%d" % u, [P, 2 * QB], U32) for u in range(UNITS)]
        w_scales = [tile("w_scales%d" % u, [P, 2 * QB], U8) for u in range(UNITS)]
        recips = tile("recips", [P, JOBS], F32)
        result = tile("result", [P, JOBS, E], F32)
        score_banks = [[ps.tile([P, PACK, QB], F32, name="score%d_%d" % (g, b)) for b in range(2)] for g in range(2)]
        y_banks = [ps.tile([P, 4, E], F32, name="y%d" % b) for b in range(4)]

        def y_of(first, count):
            if first >= 2 * LAST:
                return y_banks[first - 2 * LAST][:, 0:count, :]
            return y_banks[first // 4][:, first % 4 : first % 4 + count, :]

        def copy(engine, dst, src):
            if engine == "vector":
                nc.vector.tensor_copy(out=dst, in_=src)
            else:
                nc.scalar.copy(out=dst, in_=src)

        def quantise(codes, scales, src):
            nc.vector.quantize_mx(out=codes.bitcast(FP8X4), scales=scales, in_=src)

        def load_k(half):
            nc.sync.dma_start(out=k_raw[half][:], in_=k_view[:, :, half * N // 2 : (half + 1) * N // 2])

        def load_q(c):
            u0, u1 = Q_GROUPS[c]
            cols = slice((u0 % BLOCKS) * QB, ((u1 - 1) % BLOCKS + 1) * QB)
            heads = PAIRS[u0 // BLOCKS]
            if heads[1] == heads[0] + 1:
                src = q_rows[heads[0] * D : (heads[1] + 1) * D, :].rearrange("(p j) n -> p j n", j=PACK)
                nc.sync.dma_start(out=q_raw[c][:], in_=src[:, :, cols])
            else:
                for g, h in enumerate(heads):
                    src = q_rows[h * D : (h + 1) * D, :].rearrange("(p j) n -> p j n", j=PACK)
                    nc.sync.dma_start(out=q_raw[c][g * ROWS : (g + 1) * ROWS, :, :], in_=src[:, :, cols])

        def load_mask(c):
            nc.sync.dma_start(out=m_raw[c][:], in_=m_view[:, :, M_GROUPS[c][0] : M_GROUPS[c][1]])

        def deal_k(engine, half, s0, s1):
            dst = k_bf[:, :, half * HALF + s0 : half * HALF + s1, :].rearrange("p r s j -> p s j r")
            src = k_raw[half][:].rearrange("p j (s r) -> p s j r", r=PACK)
            copy(engine, dst, src[:, s0:s1])

        def quantise_k(half):
            s = slice(half * HALF, (half + 1) * HALF)
            for r in range(PACK):
                quantise(k_codes[:, r, s], k_scales[:, r, s], k_bf[:, r, s, :].rearrange("p s j -> p (s j)"))

        def interleave_q(engine, c):
            copy(
                engine,
                q_bf[c][:].rearrange("p (c i) j -> p c j i", i=RUN),
                q_raw[c][:].rearrange("p j (c i) -> p c j i", i=RUN),
            )

        def quantise_q(c):
            quantise(q_codes[c][:], q_scales[c][:], q_bf[c][:].rearrange("p n j -> p (n j)"))

        def interleave_v(engine):
            for g in range(KV):
                copy(
                    engine,
                    v_bf[:, g, :, :].rearrange("p (c i) r -> p c r i", i=RUN),
                    v_raw[:, g, :, :].rearrange("p r (c i) -> p c r i", i=RUN),
                )

        def quantise_v():
            quantise(v_codes[:], v_scales[:], v_bf[:].rearrange("p g e r -> p (g e r)"))

        def scale_mask(engine, c):
            q0, q1 = M_GROUPS[c]
            for r in range(PACK):
                dst, src, factor = mask_t[:, r, q0:q1], m_raw[c][:, r, :], t_sb[:, r : r + 1]
                if engine == "vector":
                    nc.vector.tensor_scalar(out=dst, in0=src, scalar1=factor, scalar2=None, op0=ALU.mult)
                else:
                    nc.scalar.activation(out=dst, in_=src, func=ACT.Copy, scale=factor)

        def scores(u):
            c = [c for c, (u0, u1) in enumerate(Q_GROUPS) if u0 <= u < u1][0]
            cols = slice((u - Q_GROUPS[c][0]) * QB, (u - Q_GROUPS[c][0] + 1) * QB)
            for r in range(PACK):
                for g in range(2):
                    rows = slice(g * ROWS, (g + 1) * ROWS)
                    nc.tensor.matmul_mx(
                        out=score_banks[g][u % 2][:, r, :],
                        lhsT=k_codes[rows, r, :].bitcast(FP8X4),
                        lhsT_scale=k_scales[rows, r, :],
                        rhs=q_codes[c][rows, cols].bitcast(FP8X4),
                        rhs_scale=q_scales[c][rows, cols],
                        start=True,
                        stop=True,
                    )

        def exponentiate(n):
            bank = score_banks[n % 2][n // 2 % 2]
            nc.scalar.activation(out=probs[n][:], in_=bank[:].rearrange("p r (c i) -> p c r i", i=RUN), func=ACT.Exp)

        def weigh(n):
            q0 = (n // 2 % BLOCKS) * QB
            nc.vector.tensor_tensor(
                out=w_bf[n // 2][:, n % 2].rearrange("p (c i) r -> p c r i", i=RUN),
                in0=probs[n][:],
                in1=mask_t[:, :, q0 : q0 + QB].rearrange("p r (c i) -> p c r i", i=RUN),
                op=ALU.mult,
            )

        def quantise_w(first, count):
            u, g = divmod(first, 2)
            cols = slice(g * QB, (g + count) * QB)
            quantise(w_codes[u][:, cols], w_scales[u][:, cols], w_bf[u][:, g : g + count].rearrange("p g n r -> p (g n r)"))

        def mix_values(first, count):
            for n in range(first, first + count):
                u, g = divmod(n, 2)
                nc.tensor.matmul_mx(
                    out=y_of(n, 1)[:, 0, :],
                    lhsT=w_codes[u][:, g * QB : (g + 1) * QB].bitcast(FP8X4),
                    lhsT_scale=w_scales[u][:, g * QB : (g + 1) * QB],
                    rhs=v_codes[:, g * E : (g + 1) * E].bitcast(FP8X4),
                    rhs_scale=v_scales[:, g * E : (g + 1) * E],
                    start=True,
                    stop=True,
                )

        def invert(first, count):
            nc.vector.reciprocal(out=recips[:, first : first + count], in_=y_of(first, count)[:, :, E - 1])

        def finish(engine, first, count):
            jobs = slice(first, first + count)
            if engine == "vector":
                factor = recips[:, jobs].unsqueeze(2).to_broadcast([P, count, E])
                nc.vector.tensor_tensor(out=result[:, jobs, :], in0=y_of(first, count), in1=factor, op=ALU.mult)
            else:
                for n in range(first, first + count):
                    nc.scalar.activation(out=result[:, n, :], in_=y_of(n, 1)[:, 0, :], func=ACT.Copy, scale=recips[:, n : n + 1])
            u, g = divmod(first, 2)
            h0, h1 = PAIRS[u // BLOCKS]
            q0 = (u % BLOCKS) * QB
            dst = out[h0 : h1 + 1 : h1 - h0, q0 : q0 + QB, :].rearrange("h q e -> q h e")
            nc.sync.dma_start(out=dst[:, g : g + count, :], in_=result[:, jobs, :])

        before_exp = {
            2: [(scale_mask, "scalar", 1)],
            5: [(interleave_q, "scalar", 3)],
            8: [(interleave_v, "scalar")],
            9: [(interleave_q, "scalar", 4)],
            12: [(finish, "scalar", 0, 2)],
            14: [(finish, "scalar", 2, 2)],
        }
        before_weigh = {
            0: [(interleave_q, "vector", 2), (scale_mask, "vector", 0), (quantise_q, 2)],
            4: [(quantise_w, 0, 2), (quantise_w, 2, 2), (scale_mask, "vector", 2), (quantise_q, 3)],
            7: [(quantise_w, 4, 2), (quantise_v,)],
            9: [(quantise_w, 6, 2), (quantise_q, 4), (invert, 0, 4)],
            12: [(quantise_w, 8, 2), (quantise_w, 10, 2)],
            14: [(invert, 4, 4), (quantise_w, 12, 1)],
            15: [(quantise_w, 13, 1), (invert, 8, 4)],
        }
        after_weigh = {
            0: [(scores, 2)],
            2: [(scores, 3)],
            4: [(scores, 4)],
            6: [(scores, 5)],
            7: [(mix_values, 0, 6)],
            9: [(scores, 6)],
            10: [(scores, 7), (mix_values, 6, 2)],
            12: [(mix_values, 8, 4)],
            14: [(mix_values, 12, 1)],
            15: [(mix_values, 13, 1)],
        }

        def run(steps):
            for fn, *args in steps:
                fn(*args)

        with tc.manual_schedule():
            nc.scalar.dma_start(out=t_sb[:], in_=t_view)

            load_k(0)
            load_q(0)
            load_k(1)
            load_q(1)
            load_q(2)
            load_mask(0)
            load_mask(1)
            load_q(3)
            load_mask(2)
            nc.sync.dma_start(out=v_raw[:], in_=v_view)
            load_q(4)

            deal_k("vector", 0, 0, HALF)
            quantise_k(0)
            interleave_q("scalar", 0)
            deal_k("vector", 1, 0, K_SHARE)
            deal_k("scalar", 1, K_SHARE, HALF)
            quantise_q(0)
            quantise_k(1)
            scores(0)
            interleave_q("scalar", 1)
            quantise_q(1)
            scores(1)
            exponentiate(0)

            for n in range(JOBS):
                if n + 1 < JOBS:
                    run(before_exp.get(n + 1, []))
                    exponentiate(n + 1)
                run(before_weigh.get(n, []))
                weigh(n)
                run(after_weigh.get(n, []))

            for u in range(2, LAST - 1):
                finish("scalar", 2 * u, 2)
            quantise_w(JOBS - 2, 1)
            mix_values(JOBS - 2, 1)
            invert(JOBS - 4, 2)
            quantise_w(JOBS - 1, 1)
            mix_values(JOBS - 1, 1)
            finish("vector", JOBS - 4, 2)
            for n in (JOBS - 2, JOBS - 1):
                invert(n, 1)
                finish("scalar", n, 1)
